import numpy as np
import ml_dtypes

BF16 = ml_dtypes.bfloat16


def bf(x):
    return np.asarray(x, np.float32).astype(BF16)


def f32(x):
    return np.asarray(x, np.float32)


def f64(x):
    return np.asarray(x).astype(np.float64)


def striped(idx):
    return np.tile(idx.reshape(-1, 16).T, (8, 1))


S, K, M, N, E, Q = 512, 128, 512, 384, 2, 192


def setup_inputs():
    return {"base": bf(np.random.standard_normal((M, S))), "x": bf(np.random.standard_normal((K, N))), "w": bf(np.random.standard_normal((E, K, M)) / np.sqrt(K)), "b": f32(0.5 * np.random.standard_normal((M, 1))), "offs": striped(np.random.permutation(S)[:N])}


def reference(base, x, w, b, offs):
    idx = offs[:16].T.reshape(-1)
    z = f64(base).copy()
    for e in range(E):
        z[:, idx[e * Q : (e + 1) * Q]] += f64(w)[e].T @ f64(x)[:, e * Q : (e + 1) * Q]
    return np.tanh(z + f64(b))

@@ -1,0 +1,68 @@
+import concourse.mybir as mybir
+from concourse.masks import make_identity
+
+P = 128
+TOKENS = 512
+FEATURES = 512
+BLOCKS = FEATURES // P
+EXPERTS = 2
+PIECE = 192
+ENTRIES = EXPERTS * PIECE
+PIECE_COLS = PIECE // 16
+
+BF16 = mybir.dt.bfloat16
+F32 = mybir.dt.float32
+U16 = mybir.dt.uint16
+
+FLOPS = 2 * P * FEATURES * ENTRIES
+
+
+def tile_scatter_matmul_kernel(tc, base, x, w, b, offs, out):
+    nc = tc.nc
+    with (
+        tc.tile_pool(name="held", bufs=1) as held,
+        tc.psum_pool(name="windows", bufs=1) as windows,
+    ):
+        offsets = held.tile([P, ENTRIES // 16], U16, name="offsets")
+        nc.sync.dma_start(offsets[:], offs)
+
+        base_tiles = []
+        for a in range(BLOCKS):
+            base_tile = held.tile([P, TOKENS], BF16, name="base%d" % a)
+            queue = nc.sync if a % 2 == 0 else nc.scalar
+            queue.dma_start(base_tile[:], base[a * P : (a + 1) * P, :])
+            base_tiles.append(base_tile)
+
+        x_tile = held.tile([P, ENTRIES], BF16, name="x_tile")
+        nc.gpsimd.dma_start(x_tile[:], x)
+        w_tile = held.tile([P, EXPERTS, FEATURES], BF16, name="w_tile")
+        nc.gpsimd.dma_start(w_tile[:], w.rearrange("e k m -> k e m"))
+
+        bias = held.tile([P, BLOCKS], F32, name="bias")
+        with nc.allow_non_contiguous_dma(reason="one float32 to a partition and block"):
+            nc.scalar.dma_start(bias[:], b.rearrange("(a p) o -> p (a o)", p=P))
+
+        ident = held.tile([P, P], BF16, name="ident")
+        make_identity(nc, ident[:])
+
+        window_tiles = []
+        for a in range(BLOCKS):
+            window = windows.tile([P, TOKENS], F32, name="window%d" % a)
+            nc.tensor.matmul(window[:], ident[:], base_tiles[a][:], start=True, stop=False)
+            window_tiles.append(window)
+
+        for a in range(BLOCKS):
+            window = window_tiles[a]
+            for e in range(EXPERTS):
+                nc.tensor.matmul(
+                    window[:].indirect(offsets[:, e * PIECE_COLS : (e + 1) * PIECE_COLS]),
+                    w_tile[:, e, a * P : (a + 1) * P],
+                    x_tile[:, e * PIECE : (e + 1) * PIECE],
+                    start=False,
+                    stop=(e == EXPERTS - 1),
+                )
+            result = held.tile([P, TOKENS], F32, name="result%d" % a)
+            nc.scalar.activation(
+                result[:], window[:], mybir.ActivationFunctionType.Tanh, bias=bias[:, a : a + 1]
+            )
+            nc.sync.dma_start(out[a * P : (a + 1) * P, :], result[:])

@@ -26,6 +26,9 @@ def tile_scatter_matmul_kernel(tc, base, x, w, b, offs, out):
         offsets = held.tile([P, ENTRIES // 16], U16, name="offsets")
         nc.sync.dma_start(offsets[:], offs)
 
+        ident = held.tile([P, P], BF16, name="ident")
+        make_identity(nc, ident[:])
+
         base_tiles = []
         for a in range(BLOCKS):
             base_tile = held.tile([P, TOKENS], BF16, name="base%d" % a)
@@ -34,16 +37,17 @@ def tile_scatter_matmul_kernel(tc, base, x, w, b, offs, out):
             base_tiles.append(base_tile)
 
         x_tile = held.tile([P, ENTRIES], BF16, name="x_tile")
-        nc.gpsimd.dma_start(x_tile[:], x)
+        nc.sync.dma_start(x_tile[:], x)
         w_tile = held.tile([P, EXPERTS, FEATURES], BF16, name="w_tile")
-        nc.gpsimd.dma_start(w_tile[:], w.rearrange("e k m -> k e m"))
+        nc.scalar.dma_start(w_tile[:], w.rearrange("e k m -> k e m"))
 
         bias = held.tile([P, BLOCKS], F32, name="bias")
         with nc.allow_non_contiguous_dma(reason="one float32 to a partition and block"):
             nc.scalar.dma_start(bias[:], b.rearrange("(a p) o -> p (a o)", p=P))
 
-        ident = held.tile([P, P], BF16, name="ident")
-        make_identity(nc, ident[:])
+        scratch = held.tile([P, 1], F32, name="scratch")
+        nc.vector.memset(scratch[:], 0.0)
+        nc.scalar.activation(scratch[:], scratch[:], mybir.ActivationFunctionType.Tanh)
 
         window_tiles = []
         for a in range(BLOCKS):

@@ -9,6 +9,7 @@ EXPERTS = 2
 PIECE = 192
 ENTRIES = EXPERTS * PIECE
 PIECE_COLS = PIECE // 16
+WARM_MATMULS = 4
 
 BF16 = mybir.dt.bfloat16
 F32 = mybir.dt.float32
@@ -25,6 +26,12 @@ def tile_scatter_matmul_kernel(tc, base, x, w, b, offs, out):
     ):
         offsets = held.tile([P, ENTRIES // 16], U16, name="offsets")
         nc.sync.dma_start(offsets[:], offs)
+
+        zeros = held.tile([P, TOKENS], BF16, name="zeros")
+        nc.vector.memset(zeros[:], 0.0)
+        spare = windows.tile([P, TOKENS], F32, name="spare")
+        for i in range(WARM_MATMULS):
+            nc.tensor.matmul(spare[:], zeros[:, 0:P], zeros[:], start=True, stop=True)
 
         ident = held.tile([P, P], BF16, name="ident")
         make_identity(nc, ident[:])

@@ -9,7 +9,6 @@ EXPERTS = 2
 PIECE = 192
 ENTRIES = EXPERTS * PIECE
 PIECE_COLS = PIECE // 16
-WARM_MATMULS = 4
 
 BF16 = mybir.dt.bfloat16
 F32 = mybir.dt.float32
@@ -27,14 +26,11 @@ def tile_scatter_matmul_kernel(tc, base, x, w, b, offs, out):
         offsets = held.tile([P, ENTRIES // 16], U16, name="offsets")
         nc.sync.dma_start(offsets[:], offs)
 
-        zeros = held.tile([P, TOKENS], BF16, name="zeros")
-        nc.vector.memset(zeros[:], 0.0)
-        spare = windows.tile([P, TOKENS], F32, name="spare")
-        for i in range(WARM_MATMULS):
-            nc.tensor.matmul(spare[:], zeros[:, 0:P], zeros[:], start=True, stop=True)
-
         ident = held.tile([P, P], BF16, name="ident")
         make_identity(nc, ident[:])
+
+        bias_rows = held.tile([BLOCKS, P], F32, name="bias_rows")
+        nc.scalar.dma_start(bias_rows[:], b.rearrange("(a p) o -> a (p o)", p=P))
 
         base_tiles = []
         for a in range(BLOCKS):
@@ -48,13 +44,16 @@ def tile_scatter_matmul_kernel(tc, base, x, w, b, offs, out):
         w_tile = held.tile([P, EXPERTS, FEATURES], BF16, name="w_tile")
         nc.scalar.dma_start(w_tile[:], w.rearrange("e k m -> k e m"))
 
-        bias = held.tile([P, BLOCKS], F32, name="bias")
-        with nc.allow_non_contiguous_dma(reason="one float32 to a partition and block"):
-            nc.scalar.dma_start(bias[:], b.rearrange("(a p) o -> p (a o)", p=P))
-
         scratch = held.tile([P, 1], F32, name="scratch")
         nc.vector.memset(scratch[:], 0.0)
         nc.scalar.activation(scratch[:], scratch[:], mybir.ActivationFunctionType.Tanh)
+
+        small_ident = held.tile([BLOCKS, BLOCKS], F32, name="small_ident")
+        make_identity(nc, small_ident[:])
+        bias_bank = windows.tile([P, BLOCKS], F32, name="bias_bank")
+        nc.tensor.matmul(bias_bank[:], bias_rows[:], small_ident[:], start=True, stop=True)
+        bias = held.tile([P, BLOCKS], F32, name="bias")
+        nc.vector.tensor_copy(bias[:], bias_bank[:])
 
         window_tiles = []
         for a in range(BLOCKS):

@@ -9,6 +9,7 @@ EXPERTS = 2
 PIECE = 192
 ENTRIES = EXPERTS * PIECE
 PIECE_COLS = PIECE // 16
+WARM_MATMULS = 3
 
 BF16 = mybir.dt.bfloat16
 F32 = mybir.dt.float32
@@ -26,11 +27,14 @@ def tile_scatter_matmul_kernel(tc, base, x, w, b, offs, out):
         offsets = held.tile([P, ENTRIES // 16], U16, name="offsets")
         nc.sync.dma_start(offsets[:], offs)
 
+        zeros = held.tile([P, TOKENS], BF16, name="zeros")
+        nc.vector.memset(zeros[:], 0.0)
+        spare = windows.tile([P, TOKENS], F32, name="spare")
+        for i in range(WARM_MATMULS):
+            nc.tensor.matmul(spare[:], zeros[:, 0:P], zeros[:], start=True, stop=True)
+
         ident = held.tile([P, P], BF16, name="ident")
         make_identity(nc, ident[:])
-
-        bias_rows = held.tile([BLOCKS, P], F32, name="bias_rows")
-        nc.scalar.dma_start(bias_rows[:], b.rearrange("(a p) o -> a (p o)", p=P))
 
         base_tiles = []
         for a in range(BLOCKS):
@@ -41,19 +45,21 @@ def tile_scatter_matmul_kernel(tc, base, x, w, b, offs, out):
 
         x_tile = held.tile([P, ENTRIES], BF16, name="x_tile")
         nc.sync.dma_start(x_tile[:], x)
-        w_tile = held.tile([P, EXPERTS, FEATURES], BF16, name="w_tile")
-        nc.scalar.dma_start(w_tile[:], w.rearrange("e k m -> k e m"))
+
+        w_tiles = []
+        for a in range(BLOCKS):
+            w_tile = held.tile([P, EXPERTS, P], BF16, name="w%d" % a)
+            queue = nc.scalar if a == 0 else nc.sync
+            queue.dma_start(w_tile[:], w[:, :, a * P : (a + 1) * P].rearrange("e k m -> k e m"))
+            w_tiles.append(w_tile)
+
+        bias = held.tile([P, BLOCKS], F32, name="bias")
+        with nc.allow_non_contiguous_dma(reason="one float32 to a partition and block"):
+            nc.scalar.dma_start(bias[:], b.rearrange("(a p) o -> p (a o)", p=P))
 
         scratch = held.tile([P, 1], F32, name="scratch")
         nc.vector.memset(scratch[:], 0.0)
         nc.scalar.activation(scratch[:], scratch[:], mybir.ActivationFunctionType.Tanh)
-
-        small_ident = held.tile([BLOCKS, BLOCKS], F32, name="small_ident")
-        make_identity(nc, small_ident[:])
-        bias_bank = windows.tile([P, BLOCKS], F32, name="bias_bank")
-        nc.tensor.matmul(bias_bank[:], bias_rows[:], small_ident[:], start=True, stop=True)
-        bias = held.tile([P, BLOCKS], F32, name="bias")
-        nc.vector.tensor_copy(bias[:], bias_bank[:])
 
         window_tiles = []
         for a in range(BLOCKS):
@@ -66,7 +72,7 @@ def tile_scatter_matmul_kernel(tc, base, x, w, b, offs, out):
             for e in range(EXPERTS):
                 nc.tensor.matmul(
                     window[:].indirect(offsets[:, e * PIECE_COLS : (e + 1) * PIECE_COLS]),
-                    w_tile[:, e, a * P : (a + 1) * P],
+                    w_tiles[a][:, e, :],
                     x_tile[:, e * PIECE : (e + 1) * PIECE],
                     start=False,
                     stop=(e == EXPERTS - 1),

@@ -24,9 +24,6 @@ def tile_scatter_matmul_kernel(tc, base, x, w, b, offs, out):
         tc.tile_pool(name="held", bufs=1) as held,
         tc.psum_pool(name="windows", bufs=1) as windows,
     ):
-        offsets = held.tile([P, ENTRIES // 16], U16, name="offsets")
-        nc.sync.dma_start(offsets[:], offs)
-
         zeros = held.tile([P, TOKENS], BF16, name="zeros")
         nc.vector.memset(zeros[:], 0.0)
         spare = windows.tile([P, TOKENS], F32, name="spare")
@@ -39,23 +36,29 @@ def tile_scatter_matmul_kernel(tc, base, x, w, b, offs, out):
         base_tiles = []
         for a in range(BLOCKS):
             base_tile = held.tile([P, TOKENS], BF16, name="base%d" % a)
-            queue = nc.sync if a % 2 == 0 else nc.scalar
-            queue.dma_start(base_tile[:], base[a * P : (a + 1) * P, :])
+            nc.sync.dma_start(base_tile[:], base[a * P : (a + 1) * P, :])
             base_tiles.append(base_tile)
+
+        offsets = held.tile([P, ENTRIES // 16], U16, name="offsets")
+        nc.sync.dma_start(offsets[:], offs)
 
         x_tile = held.tile([P, ENTRIES], BF16, name="x_tile")
         nc.sync.dma_start(x_tile[:], x)
 
-        w_tiles = []
-        for a in range(BLOCKS):
-            w_tile = held.tile([P, EXPERTS, P], BF16, name="w%d" % a)
-            queue = nc.scalar if a == 0 else nc.sync
-            queue.dma_start(w_tile[:], w[:, :, a * P : (a + 1) * P].rearrange("e k m -> k e m"))
-            w_tiles.append(w_tile)
+        w_tiles = [held.tile([P, EXPERTS, P], BF16, name="w%d" % a) for a in range(BLOCKS)]
+
+        def load_weights(a):
+            nc.sync.dma_start(w_tiles[a][:], w[:, :, a * P : (a + 1) * P].rearrange("e k m -> k e m"))
+
+        load_weights(0)
+        load_weights(1)
 
         bias = held.tile([P, BLOCKS], F32, name="bias")
         with nc.allow_non_contiguous_dma(reason="one float32 to a partition and block"):
-            nc.scalar.dma_start(bias[:], b.rearrange("(a p) o -> p (a o)", p=P))
+            nc.sync.dma_start(bias[:], b.rearrange("(a p) o -> p (a o)", p=P))
+
+        load_weights(2)
+        load_weights(3)
 
         scratch = held.tile([P, 1], F32, name="scratch")
         nc.vector.memset(scratch[:], 0.0)

@@ -80,8 +80,15 @@ def tile_scatter_matmul_kernel(tc, base, x, w, b, offs, out):
                     start=False,
                     stop=(e == EXPERTS - 1),
                 )
+            halves = 2 if a == BLOCKS - 1 else 1
+            width = TOKENS // halves
             result = held.tile([P, TOKENS], F32, name="result%d" % a)
-            nc.scalar.activation(
-                result[:], window[:], mybir.ActivationFunctionType.Tanh, bias=bias[:, a : a + 1]
-            )
-            nc.sync.dma_start(out[a * P : (a + 1) * P, :], result[:])
+            for h in range(halves):
+                columns = slice(h * width, (h + 1) * width)
+                nc.scalar.activation(
+                    result[:, columns],
+                    window[:, columns],
+                    mybir.ActivationFunctionType.Tanh,
+                    bias=bias[:, a : a + 1],
+                )
+                nc.sync.dma_start(out[a * P : (a + 1) * P, columns], result[:, columns])

@@ -9,7 +9,7 @@ EXPERTS = 2
 PIECE = 192
 ENTRIES = EXPERTS * PIECE
 PIECE_COLS = PIECE // 16
-WARM_MATMULS = 3
+WARM_MATMULS = 2
 
 BF16 = mybir.dt.bfloat16
 F32 = mybir.dt.float32
@@ -25,7 +25,7 @@ def tile_scatter_matmul_kernel(tc, base, x, w, b, offs, out):
         tc.psum_pool(name="windows", bufs=1) as windows,
     ):
         zeros = held.tile([P, TOKENS], BF16, name="zeros")
-        nc.vector.memset(zeros[:], 0.0)
+        nc.vector.memset(zeros[:].bitcast(F32), 0.0)
         spare = windows.tile([P, TOKENS], F32, name="spare")
         for i in range(WARM_MATMULS):
             nc.tensor.matmul(spare[:], zeros[:, 0:P], zeros[:], start=True, stop=True)

@@ -10,6 +10,8 @@ PIECE = 192
 ENTRIES = EXPERTS * PIECE
 PIECE_COLS = PIECE // 16
 WARM_MATMULS = 2
+SQUARE = 32
+SQUARES = P // SQUARE
 
 BF16 = mybir.dt.bfloat16
 F32 = mybir.dt.float32
@@ -29,6 +31,13 @@ def tile_scatter_matmul_kernel(tc, base, x, w, b, offs, out):
         spare = windows.tile([P, TOKENS], F32, name="spare")
         for i in range(WARM_MATMULS):
             nc.tensor.matmul(spare[:], zeros[:, 0:P], zeros[:], start=True, stop=True)
+
+        scratch = held.tile([P, 1], F32, name="scratch")
+        nc.vector.memset(scratch[:], 0.0)
+        nc.scalar.activation(scratch[:], scratch[:], mybir.ActivationFunctionType.Tanh)
+
+        bias_rows = held.tile([P, BLOCKS * SQUARE], F32, name="bias_rows", align_bytes=64)
+        nc.vector.memset(bias_rows[:], 0.0)
 
         ident = held.tile([P, P], BF16, name="ident")
         make_identity(nc, ident[:])
@@ -53,16 +62,15 @@ def tile_scatter_matmul_kernel(tc, base, x, w, b, offs, out):
         load_weights(0)
         load_weights(1)
 
-        bias = held.tile([P, BLOCKS], F32, name="bias")
-        with nc.allow_non_contiguous_dma(reason="one float32 to a partition and block"):
-            nc.sync.dma_start(bias[:], b.rearrange("(a p) o -> p (a o)", p=P))
+        nc.sync.dma_start(
+            bias_rows[0:P:SQUARE, :].rearrange("i (a r) -> i a r", r=SQUARE),
+            b.rearrange("(a i r) o -> i a (r o)", a=BLOCKS, i=SQUARES),
+        )
+        bias = held.tile([P, BLOCKS * SQUARE], F32, name="bias", align_bytes=64)
+        nc.vector.transpose(bias[:], bias_rows[:])
 
         load_weights(2)
         load_weights(3)
-
-        scratch = held.tile([P, 1], F32, name="scratch")
-        nc.vector.memset(scratch[:], 0.0)
-        nc.scalar.activation(scratch[:], scratch[:], mybir.ActivationFunctionType.Tanh)
 
         window_tiles = []
         for a in range(BLOCKS):
@@ -89,6 +97,6 @@ def tile_scatter_matmul_kernel(tc, base, x, w, b, offs, out):
                     result[:, columns],
                     window[:, columns],
                     mybir.ActivationFunctionType.Tanh,
-                    bias=bias[:, a : a + 1],
+                    bias=bias[:, a * SQUARE : a * SQUARE + 1],
                 )
                 nc.sync.dma_start(out[a * P : (a + 1) * P, columns], result[:, columns])

@@ -12,6 +12,8 @@ PIECE_COLS = PIECE // 16
 WARM_MATMULS = 2
 SQUARE = 32
 SQUARES = P // SQUARE
+FILL_PIECE = 64
+FILL_PIECES = TOKENS // FILL_PIECE
 
 BF16 = mybir.dt.bfloat16
 F32 = mybir.dt.float32
@@ -37,16 +39,20 @@ def tile_scatter_matmul_kernel(tc, base, x, w, b, offs, out):
         nc.scalar.activation(scratch[:], scratch[:], mybir.ActivationFunctionType.Tanh)
 
         bias_rows = held.tile([P, BLOCKS * SQUARE], F32, name="bias_rows", align_bytes=64)
-        nc.vector.memset(bias_rows[:], 0.0)
-
+        nc.gpsimd.memset(bias_rows[:], 0.0)
         ident = held.tile([P, P], BF16, name="ident")
         make_identity(nc, ident[:])
 
-        base_tiles = []
-        for a in range(BLOCKS):
-            base_tile = held.tile([P, TOKENS], BF16, name="base%d" % a)
-            nc.sync.dma_start(base_tile[:], base[a * P : (a + 1) * P, :])
-            base_tiles.append(base_tile)
+        base_tiles = [held.tile([P, TOKENS], BF16, name="base%d" % a) for a in range(BLOCKS)]
+        w_tiles = [held.tile([P, EXPERTS, P], BF16, name="w%d" % a) for a in range(BLOCKS)]
+
+        def load_base(a):
+            nc.sync.dma_start(base_tiles[a][:], base[a * P : (a + 1) * P, :])
+
+        def load_weights(a):
+            nc.sync.dma_start(w_tiles[a][:], w[:, :, a * P : (a + 1) * P].rearrange("e k m -> k e m"))
+
+        load_base(0)
 
         offsets = held.tile([P, ENTRIES // 16], U16, name="offsets")
         nc.sync.dma_start(offsets[:], offs)
@@ -54,13 +60,7 @@ def tile_scatter_matmul_kernel(tc, base, x, w, b, offs, out):
         x_tile = held.tile([P, ENTRIES], BF16, name="x_tile")
         nc.sync.dma_start(x_tile[:], x)
 
-        w_tiles = [held.tile([P, EXPERTS, P], BF16, name="w%d" % a) for a in range(BLOCKS)]
-
-        def load_weights(a):
-            nc.sync.dma_start(w_tiles[a][:], w[:, :, a * P : (a + 1) * P].rearrange("e k m -> k e m"))
-
         load_weights(0)
-        load_weights(1)
 
         nc.sync.dma_start(
             bias_rows[0:P:SQUARE, :].rearrange("i (a r) -> i a r", r=SQUARE),
@@ -69,16 +69,22 @@ def tile_scatter_matmul_kernel(tc, base, x, w, b, offs, out):
         bias = held.tile([P, BLOCKS * SQUARE], F32, name="bias", align_bytes=64)
         nc.vector.transpose(bias[:], bias_rows[:])
 
-        load_weights(2)
-        load_weights(3)
+        for a in range(1, BLOCKS):
+            load_base(a)
+        for a in range(1, BLOCKS):
+            load_weights(a)
 
-        window_tiles = []
-        for a in range(BLOCKS):
-            window = windows.tile([P, TOKENS], F32, name="window%d" % a)
-            nc.tensor.matmul(window[:], ident[:], base_tiles[a][:], start=True, stop=False)
-            window_tiles.append(window)
+        window_tiles = [windows.tile([P, TOKENS], F32, name="window%d" % a) for a in range(BLOCKS)]
 
-        for a in range(BLOCKS):
+        def fill(a, pieces):
+            width = TOKENS // pieces
+            for j in range(pieces):
+                columns = slice(j * width, (j + 1) * width)
+                nc.tensor.matmul(
+                    window_tiles[a][:, columns], ident[:], base_tiles[a][:, columns], start=(j == 0), stop=False
+                )
+
+        def scatter_and_finish(a):
             window = window_tiles[a]
             for e in range(EXPERTS):
                 nc.tensor.matmul(
@@ -100,3 +106,10 @@ def tile_scatter_matmul_kernel(tc, base, x, w, b, offs, out):
                     bias=bias[:, a * SQUARE : a * SQUARE + 1],
                 )
                 nc.sync.dma_start(out[a * P : (a + 1) * P, columns], result[:, columns])
+
+        fill(0, 1)
+        scatter_and_finish(0)
+        for a in range(1, BLOCKS):
+            fill(a, FILL_PIECES)
+        for a in range(1, BLOCKS):
+            scatter_and_finish(a)

@@ -12,8 +12,7 @@ PIECE_COLS = PIECE // 16
 WARM_MATMULS = 2
 SQUARE = 32
 SQUARES = P // SQUARE
-FILL_PIECE = 64
-FILL_PIECES = TOKENS // FILL_PIECE
+FIRST_RUN = 2
 
 BF16 = mybir.dt.bfloat16
 F32 = mybir.dt.float32
@@ -52,7 +51,8 @@ def tile_scatter_matmul_kernel(tc, base, x, w, b, offs, out):
         def load_weights(a):
             nc.sync.dma_start(w_tiles[a][:], w[:, :, a * P : (a + 1) * P].rearrange("e k m -> k e m"))
 
-        load_base(0)
+        for a in range(FIRST_RUN):
+            load_base(a)
 
         offsets = held.tile([P, ENTRIES // 16], U16, name="offsets")
         nc.sync.dma_start(offsets[:], offs)
@@ -69,9 +69,11 @@ def tile_scatter_matmul_kernel(tc, base, x, w, b, offs, out):
         bias = held.tile([P, BLOCKS * SQUARE], F32, name="bias", align_bytes=64)
         nc.vector.transpose(bias[:], bias_rows[:])
 
-        for a in range(1, BLOCKS):
+        for a in range(1, FIRST_RUN):
+            load_weights(a)
+        for a in range(FIRST_RUN, BLOCKS):
             load_base(a)
-        for a in range(1, BLOCKS):
+        for a in range(FIRST_RUN, BLOCKS):
             load_weights(a)
 
         window_tiles = [windows.tile([P, TOKENS], F32, name="window%d" % a) for a in range(BLOCKS)]
@@ -107,9 +109,11 @@ def tile_scatter_matmul_kernel(tc, base, x, w, b, offs, out):
                 )
                 nc.sync.dma_start(out[a * P : (a + 1) * P, columns], result[:, columns])
 
-        fill(0, 1)
-        scatter_and_finish(0)
-        for a in range(1, BLOCKS):
-            fill(a, FILL_PIECES)
-        for a in range(1, BLOCKS):
+        for a in range(FIRST_RUN):
+            fill(a, 1)
+        for a in range(FIRST_RUN):
+            scatter_and_finish(a)
+        fill(FIRST_RUN, 16)
+        fill(FIRST_RUN + 1, 8)
+        for a in range(FIRST_RUN, BLOCKS):
             scatter_and_finish(a)

@@ -43,7 +43,8 @@ def tile_scatter_matmul_kernel(tc, base, x, w, b, offs, out):
         make_identity(nc, ident[:])
 
         base_tiles = [held.tile([P, TOKENS], BF16, name="base%d" % a) for a in range(BLOCKS)]
-        w_tiles = [held.tile([P, EXPERTS, P], BF16, name="w%d" % a) for a in range(BLOCKS)]
+        w_tiles = [held.tile([P, EXPERTS, P], BF16, name="w%d" % a) for a in range(FIRST_RUN)]
+        w_late = held.tile([P, EXPERTS, FEATURES - FIRST_RUN * P], BF16, name="w_late")
 
         def load_base(a):
             nc.sync.dma_start(base_tiles[a][:], base[a * P : (a + 1) * P, :])
@@ -51,16 +52,25 @@ def tile_scatter_matmul_kernel(tc, base, x, w, b, offs, out):
         def load_weights(a):
             nc.sync.dma_start(w_tiles[a][:], w[:, :, a * P : (a + 1) * P].rearrange("e k m -> k e m"))
 
+        def weights(a, e):
+            if a < FIRST_RUN:
+                return w_tiles[a][:, e, :]
+            return w_late[:, e, (a - FIRST_RUN) * P : (a - FIRST_RUN + 1) * P]
+
         for a in range(FIRST_RUN):
             load_base(a)
 
         offsets = held.tile([P, ENTRIES // 16], U16, name="offsets")
         nc.sync.dma_start(offsets[:], offs)
 
-        x_tile = held.tile([P, ENTRIES], BF16, name="x_tile")
-        nc.sync.dma_start(x_tile[:], x)
+        x_tiles = [held.tile([P, PIECE], BF16, name="x%d" % e) for e in range(EXPERTS)]
 
+        def load_x(e):
+            nc.sync.dma_start(x_tiles[e][:], x[:, e * PIECE : (e + 1) * PIECE])
+
+        load_x(0)
         load_weights(0)
+        load_x(1)
 
         nc.sync.dma_start(
             bias_rows[0:P:SQUARE, :].rearrange("i (a r) -> i a r", r=SQUARE),
@@ -73,8 +83,7 @@ def tile_scatter_matmul_kernel(tc, base, x, w, b, offs, out):
             load_weights(a)
         for a in range(FIRST_RUN, BLOCKS):
             load_base(a)
-        for a in range(FIRST_RUN, BLOCKS):
-            load_weights(a)
+        nc.sync.dma_start(w_late[:], w[:, :, FIRST_RUN * P :].rearrange("e k m -> k e m"))
 
         window_tiles = [windows.tile([P, TOKENS], F32, name="window%d" % a) for a in range(BLOCKS)]
 
@@ -91,8 +100,8 @@ def tile_scatter_matmul_kernel(tc, base, x, w, b, offs, out):
             for e in range(EXPERTS):
                 nc.tensor.matmul(
                     window[:].indirect(offsets[:, e * PIECE_COLS : (e + 1) * PIECE_COLS]),
-                    w_tiles[a][:, e, :],
-                    x_tile[:, e * PIECE : (e + 1) * PIECE],
+                    weights(a, e),
+                    x_tiles[e][:],
                     start=False,
                     stop=(e == EXPERTS - 1),
                 )

@@ -27,11 +27,17 @@ def tile_scatter_matmul_kernel(tc, base, x, w, b, offs, out):
         tc.tile_pool(name="held", bufs=1) as held,
         tc.psum_pool(name="windows", bufs=1) as windows,
     ):
-        zeros = held.tile([P, TOKENS], BF16, name="zeros")
-        nc.vector.memset(zeros[:].bitcast(F32), 0.0)
+        zeros = held.tile([P, P], BF16, name="zeros")
+        nc.gpsimd.memset(zeros[:].bitcast(F32), 0.0)
         spare = windows.tile([P, TOKENS], F32, name="spare")
         for i in range(WARM_MATMULS):
-            nc.tensor.matmul(spare[:], zeros[:, 0:P], zeros[:], start=True, stop=True)
+            nc.tensor.matmul(
+                spare[:].rearrange("p (r c) -> p r c", c=P),
+                zeros[:],
+                zeros[:].unsqueeze(1).to_broadcast([P, TOKENS // P, P]),
+                start=True,
+                stop=True,
+            )
 
         scratch = held.tile([P, 1], F32, name="scratch")
         nc.vector.memset(scratch[:], 0.0)

@@ -9,6 +9,7 @@ EXPERTS = 2
 PIECE = 192
 ENTRIES = EXPERTS * PIECE
 PIECE_COLS = PIECE // 16
+X_CUT = 256
 WARM_MATMULS = 2
 SQUARE = 32
 SQUARES = P // SQUARE
@@ -69,14 +70,14 @@ def tile_scatter_matmul_kernel(tc, base, x, w, b, offs, out):
         offsets = held.tile([P, ENTRIES // 16], U16, name="offsets")
         nc.sync.dma_start(offsets[:], offs)
 
-        x_tiles = [held.tile([P, PIECE], BF16, name="x%d" % e) for e in range(EXPERTS)]
+        x_tile = held.tile([P, ENTRIES], BF16, name="x_tile")
 
-        def load_x(e):
-            nc.sync.dma_start(x_tiles[e][:], x[:, e * PIECE : (e + 1) * PIECE])
+        def load_x(first, last):
+            nc.sync.dma_start(x_tile[:, first:last], x[:, first:last])
 
-        load_x(0)
+        load_x(0, X_CUT)
         load_weights(0)
-        load_x(1)
+        load_x(X_CUT, ENTRIES)
 
         nc.sync.dma_start(
             bias_rows[0:P:SQUARE, :].rearrange("i (a r) -> i a r", r=SQUARE),
@@ -107,7 +108,7 @@ def tile_scatter_matmul_kernel(tc, base, x, w, b, offs, out):
                 nc.tensor.matmul(
                     window[:].indirect(offsets[:, e * PIECE_COLS : (e + 1) * PIECE_COLS]),
                     weights(a, e),
-                    x_tiles[e][:],
+                    x_tile[:, e * PIECE : (e + 1) * PIECE],
                     start=False,
                     stop=(e == EXPERTS - 1),
                 )

@@ -14,6 +14,7 @@ WARM_MATMULS = 2
 SQUARE = 32
 SQUARES = P // SQUARE
 FIRST_RUN = 2
+FILL_WIDTH = 44
 
 BF16 = mybir.dt.bfloat16
 F32 = mybir.dt.float32
@@ -50,18 +51,18 @@ def tile_scatter_matmul_kernel(tc, base, x, w, b, offs, out):
         make_identity(nc, ident[:])
 
         base_tiles = [held.tile([P, TOKENS], BF16, name="base%d" % a) for a in range(BLOCKS)]
-        w_tiles = [held.tile([P, EXPERTS, P], BF16, name="w%d" % a) for a in range(FIRST_RUN)]
+        w_tiles = [held.tile([P, FIRST_RUN * P], BF16, name="w_expert%d" % e) for e in range(EXPERTS)]
         w_late = held.tile([P, EXPERTS, FEATURES - FIRST_RUN * P], BF16, name="w_late")
 
         def load_base(a):
             nc.sync.dma_start(base_tiles[a][:], base[a * P : (a + 1) * P, :])
 
-        def load_weights(a):
-            nc.sync.dma_start(w_tiles[a][:], w[:, :, a * P : (a + 1) * P].rearrange("e k m -> k e m"))
+        def load_weights(e):
+            nc.sync.dma_start(w_tiles[e][:], w[e, :, : FIRST_RUN * P])
 
         def weights(a, e):
             if a < FIRST_RUN:
-                return w_tiles[a][:, e, :]
+                return w_tiles[e][:, a * P : (a + 1) * P]
             return w_late[:, e, (a - FIRST_RUN) * P : (a - FIRST_RUN + 1) * P]
 
         for a in range(FIRST_RUN):
@@ -78,6 +79,7 @@ def tile_scatter_matmul_kernel(tc, base, x, w, b, offs, out):
         load_x(0, X_CUT)
         load_weights(0)
         load_x(X_CUT, ENTRIES)
+        load_weights(1)
 
         nc.sync.dma_start(
             bias_rows[0:P:SQUARE, :].rearrange("i (a r) -> i a r", r=SQUARE),
@@ -86,32 +88,30 @@ def tile_scatter_matmul_kernel(tc, base, x, w, b, offs, out):
         bias = held.tile([P, BLOCKS * SQUARE], F32, name="bias", align_bytes=64)
         nc.vector.transpose(bias[:], bias_rows[:])
 
-        for a in range(1, FIRST_RUN):
-            load_weights(a)
         for a in range(FIRST_RUN, BLOCKS):
             load_base(a)
         nc.sync.dma_start(w_late[:], w[:, :, FIRST_RUN * P :].rearrange("e k m -> k e m"))
 
         window_tiles = [windows.tile([P, TOKENS], F32, name="window%d" % a) for a in range(BLOCKS)]
 
-        def fill(a, pieces):
-            width = TOKENS // pieces
-            for j in range(pieces):
-                columns = slice(j * width, (j + 1) * width)
+        def fill(a, width):
+            for first in range(0, TOKENS, width):
+                columns = slice(first, min(first + width, TOKENS))
                 nc.tensor.matmul(
-                    window_tiles[a][:, columns], ident[:], base_tiles[a][:, columns], start=(j == 0), stop=False
+                    window_tiles[a][:, columns], ident[:], base_tiles[a][:, columns], start=(first == 0), stop=False
                 )
 
-        def scatter_and_finish(a):
+        def scatter(a, e):
+            nc.tensor.matmul(
+                window_tiles[a][:].indirect(offsets[:, e * PIECE_COLS : (e + 1) * PIECE_COLS]),
+                weights(a, e),
+                x_tile[:, e * PIECE : (e + 1) * PIECE],
+                start=False,
+                stop=(e == EXPERTS - 1),
+            )
+
+        def finish(a):
             window = window_tiles[a]
-            for e in range(EXPERTS):
-                nc.tensor.matmul(
-                    window[:].indirect(offsets[:, e * PIECE_COLS : (e + 1) * PIECE_COLS]),
-                    weights(a, e),
-                    x_tile[:, e * PIECE : (e + 1) * PIECE],
-                    start=False,
-                    stop=(e == EXPERTS - 1),
-                )
             halves = 2 if a == BLOCKS - 1 else 1
             width = TOKENS // halves
             result = held.tile([P, TOKENS], F32, name="result%d" % a)
@@ -126,10 +126,15 @@ def tile_scatter_matmul_kernel(tc, base, x, w, b, offs, out):
                 nc.sync.dma_start(out[a * P : (a + 1) * P, columns], result[:, columns])
 
         for a in range(FIRST_RUN):
-            fill(a, 1)
+            fill(a, TOKENS)
+        for e in range(EXPERTS):
+            for a in range(FIRST_RUN):
+                scatter(a, e)
         for a in range(FIRST_RUN):
-            scatter_and_finish(a)
-        fill(FIRST_RUN, 16)
-        fill(FIRST_RUN + 1, 8)
+            finish(a)
         for a in range(FIRST_RUN, BLOCKS):
-            scatter_and_finish(a)
+            fill(a, FILL_WIDTH)
+        for a in range(FIRST_RUN, BLOCKS):
+            for e in range(EXPERTS):
+                scatter(a, e)
+            finish(a)

@@ -65,11 +65,13 @@ def tile_scatter_matmul_kernel(tc, base, x, w, b, offs, out):
                 return w_tiles[e][:, a * P : (a + 1) * P]
             return w_late[:, e, (a - FIRST_RUN) * P : (a - FIRST_RUN + 1) * P]
 
-        for a in range(FIRST_RUN):
-            load_base(a)
+        load_base(0)
 
         offsets = held.tile([P, ENTRIES // 16], U16, name="offsets")
         nc.sync.dma_start(offsets[:], offs)
+
+        for a in range(1, FIRST_RUN):
+            load_base(a)
 
         x_tile = held.tile([P, ENTRIES], BF16, name="x_tile")
 
@@ -81,6 +83,8 @@ def tile_scatter_matmul_kernel(tc, base, x, w, b, offs, out):
         load_x(X_CUT, ENTRIES)
         load_weights(1)
 
+        load_base(FIRST_RUN)
+
         nc.sync.dma_start(
             bias_rows[0:P:SQUARE, :].rearrange("i (a r) -> i a r", r=SQUARE),
             b.rearrange("(a i r) o -> i a (r o)", a=BLOCKS, i=SQUARES),
@@ -88,7 +92,7 @@ def tile_scatter_matmul_kernel(tc, base, x, w, b, offs, out):
         bias = held.tile([P, BLOCKS * SQUARE], F32, name="bias", align_bytes=64)
         nc.vector.transpose(bias[:], bias_rows[:])
 
-        for a in range(FIRST_RUN, BLOCKS):
+        for a in range(FIRST_RUN + 1, BLOCKS):
             load_base(a)
         nc.sync.dma_start(w_late[:], w[:, :, FIRST_RUN * P :].rearrange("e k m -> k e m"))
 

@@ -11,6 +11,7 @@ ENTRIES = EXPERTS * PIECE
 PIECE_COLS = PIECE // 16
 X_CUT = 256
 WARM_MATMULS = 2
+WARM_WIDTH = 32
 SQUARE = 32
 SQUARES = P // SQUARE
 FIRST_RUN = 2
@@ -29,14 +30,14 @@ def tile_scatter_matmul_kernel(tc, base, x, w, b, offs, out):
         tc.tile_pool(name="held", bufs=1) as held,
         tc.psum_pool(name="windows", bufs=1) as windows,
     ):
-        zeros = held.tile([P, P], BF16, name="zeros")
+        zeros = held.tile([P, WARM_WIDTH], BF16, name="zeros")
         nc.gpsimd.memset(zeros[:].bitcast(F32), 0.0)
         spare = windows.tile([P, TOKENS], F32, name="spare")
         for i in range(WARM_MATMULS):
             nc.tensor.matmul(
-                spare[:].rearrange("p (r c) -> p r c", c=P),
+                spare[:WARM_WIDTH, :].rearrange("p (r c) -> p r c", c=WARM_WIDTH),
                 zeros[:],
-                zeros[:].unsqueeze(1).to_broadcast([P, TOKENS // P, P]),
+                zeros[:].unsqueeze(1).to_broadcast([P, TOKENS // WARM_WIDTH, WARM_WIDTH]),
                 start=True,
                 stop=True,
             )

@@ -10,7 +10,7 @@ PIECE = 192
 ENTRIES = EXPERTS * PIECE
 PIECE_COLS = PIECE // 16
 X_CUT = 256
-WARM_MATMULS = 2
+WARM_ROUNDS = 2
 WARM_WIDTH = 32
 SQUARE = 32
 SQUARES = P // SQUARE
@@ -33,14 +33,15 @@ def tile_scatter_matmul_kernel(tc, base, x, w, b, offs, out):
         zeros = held.tile([P, WARM_WIDTH], BF16, name="zeros")
         nc.gpsimd.memset(zeros[:].bitcast(F32), 0.0)
         spare = windows.tile([P, TOKENS], F32, name="spare")
-        for i in range(WARM_MATMULS):
-            nc.tensor.matmul(
-                spare[:WARM_WIDTH, :].rearrange("p (r c) -> p r c", c=WARM_WIDTH),
-                zeros[:],
-                zeros[:].unsqueeze(1).to_broadcast([P, TOKENS // WARM_WIDTH, WARM_WIDTH]),
-                start=True,
-                stop=True,
-            )
+        for i in range(WARM_ROUNDS):
+            for first in range(0, P, WARM_WIDTH):
+                nc.tensor.matmul(
+                    spare[first : first + WARM_WIDTH, :].rearrange("p (r c) -> p r c", c=WARM_WIDTH),
+                    zeros[:],
+                    zeros[:].unsqueeze(1).to_broadcast([P, TOKENS // WARM_WIDTH, WARM_WIDTH]),
+                    start=True,
+                    stop=True,
+                )
 
         scratch = held.tile([P, 1], F32, name="scratch")
         nc.vector.memset(scratch[:], 0.0)

import concourse.mybir as mybir
from concourse.masks import make_identity

P = 128
TOKENS = 512
FEATURES = 512
BLOCKS = FEATURES // P
EXPERTS = 2
PIECE = 192
ENTRIES = EXPERTS * PIECE
PIECE_COLS = PIECE // 16
X_CUT = 256
WARM_ROUNDS = 2
WARM_WIDTH = 32
SQUARE = 32
SQUARES = P // SQUARE
FIRST_RUN = 2
FILL_WIDTH = 44

BF16 = mybir.dt.bfloat16
F32 = mybir.dt.float32
U16 = mybir.dt.uint16

FLOPS = 2 * P * FEATURES * ENTRIES


def tile_scatter_matmul_kernel(tc, base, x, w, b, offs, out):
    nc = tc.nc
    with (
        tc.tile_pool(name="held", bufs=1) as held,
        tc.psum_pool(name="windows", bufs=1) as windows,
    ):
        zeros = held.tile([P, WARM_WIDTH], BF16, name="zeros")
        nc.gpsimd.memset(zeros[:].bitcast(F32), 0.0)
        spare = windows.tile([P, TOKENS], F32, name="spare")
        for i in range(WARM_ROUNDS):
            for first in range(0, P, WARM_WIDTH):
                nc.tensor.matmul(
                    spare[first : first + WARM_WIDTH, :].rearrange("p (r c) -> p r c", c=WARM_WIDTH),
                    zeros[:],
                    zeros[:].unsqueeze(1).to_broadcast([P, TOKENS // WARM_WIDTH, WARM_WIDTH]),
                    start=True,
                    stop=True,
                )

        scratch = held.tile([P, 1], F32, name="scratch")
        nc.vector.memset(scratch[:], 0.0)
        nc.scalar.activation(scratch[:], scratch[:], mybir.ActivationFunctionType.Tanh)

        bias_rows = held.tile([P, BLOCKS * SQUARE], F32, name="bias_rows", align_bytes=64)
        nc.gpsimd.memset(bias_rows[:], 0.0)
        ident = held.tile([P, P], BF16, name="ident")
        make_identity(nc, ident[:])

        base_tiles = [held.tile([P, TOKENS], BF16, name="base%d" % a) for a in range(BLOCKS)]
        w_tiles = [held.tile([P, FIRST_RUN * P], BF16, name="w_expert%d" % e) for e in range(EXPERTS)]
        w_late = held.tile([P, EXPERTS, FEATURES - FIRST_RUN * P], BF16, name="w_late")

        def load_base(a):
            nc.sync.dma_start(base_tiles[a][:], base[a * P : (a + 1) * P, :])

        def load_weights(e):
            nc.sync.dma_start(w_tiles[e][:], w[e, :, : FIRST_RUN * P])

        def weights(a, e):
            if a < FIRST_RUN:
                return w_tiles[e][:, a * P : (a + 1) * P]
            return w_late[:, e, (a - FIRST_RUN) * P : (a - FIRST_RUN + 1) * P]

        load_base(0)

        offsets = held.tile([P, ENTRIES // 16], U16, name="offsets")
        nc.sync.dma_start(offsets[:], offs)

        for a in range(1, FIRST_RUN):
            load_base(a)

        x_tile = held.tile([P, ENTRIES], BF16, name="x_tile")

        def load_x(first, last):
            nc.sync.dma_start(x_tile[:, first:last], x[:, first:last])

        load_x(0, X_CUT)
        load_weights(0)
        load_x(X_CUT, ENTRIES)
        load_weights(1)

        load_base(FIRST_RUN)

        nc.sync.dma_start(
            bias_rows[0:P:SQUARE, :].rearrange("i (a r) -> i a r", r=SQUARE),
            b.rearrange("(a i r) o -> i a (r o)", a=BLOCKS, i=SQUARES),
        )
        bias = held.tile([P, BLOCKS * SQUARE], F32, name="bias", align_bytes=64)
        nc.vector.transpose(bias[:], bias_rows[:])

        for a in range(FIRST_RUN + 1, BLOCKS):
            load_base(a)
        nc.sync.dma_start(w_late[:], w[:, :, FIRST_RUN * P :].rearrange("e k m -> k e m"))

        window_tiles = [windows.tile([P, TOKENS], F32, name="window%d" % a) for a in range(BLOCKS)]

        def fill(a, width):
            for first in range(0, TOKENS, width):
                columns = slice(first, min(first + width, TOKENS))
                nc.tensor.matmul(
                    window_tiles[a][:, columns], ident[:], base_tiles[a][:, columns], start=(first == 0), stop=False
                )

        def scatter(a, e):
            nc.tensor.matmul(
                window_tiles[a][:].indirect(offsets[:, e * PIECE_COLS : (e + 1) * PIECE_COLS]),
                weights(a, e),
                x_tile[:, e * PIECE : (e + 1) * PIECE],
                start=False,
                stop=(e == EXPERTS - 1),
            )

        def finish(a):
            window = window_tiles[a]
            halves = 2 if a == BLOCKS - 1 else 1
            width = TOKENS // halves
            result = held.tile([P, TOKENS], F32, name="result%d" % a)
            for h in range(halves):
                columns = slice(h * width, (h + 1) * width)
                nc.scalar.activation(
                    result[:, columns],
                    window[:, columns],
                    mybir.ActivationFunctionType.Tanh,
                    bias=bias[:, a * SQUARE : a * SQUARE + 1],
                )
                nc.sync.dma_start(out[a * P : (a + 1) * P, columns], result[:, columns])

        for a in range(FIRST_RUN):
            fill(a, TOKENS)
        for e in range(EXPERTS):
            for a in range(FIRST_RUN):
                scatter(a, e)
        for a in range(FIRST_RUN):
            finish(a)
        for a in range(FIRST_RUN, BLOCKS):
            fill(a, FILL_WIDTH)
        for a in range(FIRST_RUN, BLOCKS):
            for e in range(EXPERTS):
                scatter(a, e)
            finish(a)
